import numpy as np
import ml_dtypes


def mxq(x, axis, fmt="e4m3"):
    dtype, down = {"e4m3": (ml_dtypes.float8_e4m3fn, 7), "e5m2": (ml_dtypes.float8_e5m2, 14)}[fmt]
    v = np.moveaxis(np.asarray(x, np.float32).astype(ml_dtypes.bfloat16).astype(np.float64), axis, -1)
    blocks = v.reshape(v.shape[:-1] + (-1, 32))
    amax = np.abs(blocks).max(-1, keepdims=True)
    byte = np.maximum(np.where(amax > 0, np.frexp(amax)[1] - 1 + 127, 0) - down, 1)
    scale = np.exp2(byte - 127.0)
    codes = (blocks / scale).astype(np.float32).astype(dtype).astype(np.float64)
    return np.moveaxis((codes * scale).reshape(v.shape), -1, axis)


WIDE = False


def mx_kscale(k):
    if not WIDE:
        return np.ones(k)
    levels = np.array([10, -10, 5, -5, 0])
    if k % 512:
        return np.exp2(np.random.permutation(np.resize(levels, k // 32))).repeat(32)
    a = np.empty((k // 512, 16))
    for p in range(k // 512):
        a[p, :8] = np.random.permutation(np.resize(levels, 8))
        for g in range(8):
            far = levels[np.abs(levels - a[p, g]) >= 10]
            a[p, g + 8] = far[np.random.randint(len(far))]
    return np.exp2(a.ravel()).repeat(32)


def f64(x):
    return np.asarray(x).astype(np.float64)


def striped(idx):
    return np.tile(np.asarray(idx).reshape(-1, 16).T, (8, 1)).astype(np.uint16)


def unstriped(offs):
    return offs[:16].T.reshape(-1).astype(np.int64)


E2M1 = np.array([0.0, 0.5, 1.0, 1.5, 2.0, 3.0, 4.0, 6.0, -0.0, -0.5, -1.0, -1.5, -2.0, -3.0, -4.0, -6.0])


def pack_weight(w, fmt):
    k, n = w.shape
    w = f64(np.asarray(w, np.float32).astype(ml_dtypes.bfloat16)).reshape(k // 32, 32, n)
    amax = np.abs(w).max(1)
    if fmt == "e4m3":
        byte = np.frexp(amax)[1] - 1 + 127 - 7
    else:
        mant, ex = np.frexp(amax / 6.0)
        byte = np.where(mant > 0.5, ex, ex - 1) + 127
    byte = np.clip(np.where(amax > 0, byte, 1), 1, 254)
    scaled = (w * np.exp2(127.0 - byte)[:, None, :]).reshape(k, n).astype(np.float32)
    by_word = np.ascontiguousarray(scaled.reshape(k // 512, 128, 4, n).transpose(0, 1, 3, 2))
    if fmt == "e4m3":
        words = by_word.astype(ml_dtypes.float8_e4m3fn).view(np.uint8)
    else:
        c = by_word.astype(ml_dtypes.float4_e2m1fn).view(np.uint8) & 0xF
        words = (c[..., 0::2] | (c[..., 1::2] << 4)).reshape(k // 512, 128, 2 * n)
    return np.ascontiguousarray(words), np.ascontiguousarray(byte.astype(np.uint8).reshape(k // 512, 16, n))


def unpack_weight(words, scales, fmt):
    g, _, n = scales.shape
    words = np.ascontiguousarray(words).reshape(g, 128, n, -1)
    if fmt == "e4m3":
        vals = words.view(ml_dtypes.float8_e4m3fn).astype(np.float64)
    else:
        nib = np.empty((g, 128, n, 4), np.uint8)
        nib[..., 0::2] = words & 0xF
        nib[..., 1::2] = words >> 4
        vals = E2M1[nib]
    vals = vals * np.repeat(np.exp2(scales.astype(np.float64) - 127.0), 8, axis=1)[..., None]
    return vals.transpose(0, 1, 3, 2).reshape(g * 512, n)


K, S, T, N = 1024, 512, 512, 512


def setup_inputs():
    n = np.random.standard_normal
    idx = np.random.randint(0, S, T)
    idx2 = np.random.randint(0, S, T)
    fk = mx_kscale(K)
    xbp = pack_weight(n((K, S)) / fk[:, None], "e4m3")
    return {
        "xb_words": xbp[0],
        "xb_scales": xbp[1],
        "wa": (n((K, N)) * 1 / np.sqrt(K) * fk[:, None]).astype(np.float32),
        "ga": (np.random.uniform(0.4, 1.0, (1, T))).astype(np.float32),
        "offs": striped(idx),
        "offs2": striped(idx2),
    }


def reference(xb_words, xb_scales, wa, ga, offs, offs2):
    idx = unstriped(offs)
    idx2 = unstriped(offs2)
    xbu = unpack_weight(xb_words, xb_scales, "e4m3")
    waq = mxq(f64(wa), 0, "e4m3")
    z = waq.T @ xbu
    y = f64(ga) * z[:, idx] / (1.0 + np.abs(z[:, idx] - z[:, idx2]))
    return y

@@ -1,0 +1,185 @@
+from contextlib import ExitStack
+
+import concourse.mybir as mybir
+from concourse.masks import make_identity
+
+K, S, T, N = 1024, 512, 512, 512
+FLOPS = 2 * K * S * N
+
+F32 = mybir.dt.float32
+BF16 = mybir.dt.bfloat16
+I32 = mybir.dt.int32
+U32 = mybir.dt.uint32
+U16 = mybir.dt.uint16
+U8 = mybir.dt.uint8
+FP8X4 = mybir.dt.float8_e4m3fn_x4
+ACT = mybir.ActivationFunctionType
+ALU = mybir.AluOpType
+
+P = 128
+PACK = 4
+K_PASS = P * PACK
+PASSES = K // K_PASS
+BLOCKS = N // P
+HALF = T // 2
+LIST_COLS = HALF // 16
+HALVES = [(slice(h * HALF, (h + 1) * HALF), slice(h * LIST_COLS, (h + 1) * LIST_COLS)) for h in range(2)]
+
+
+def tile_moe_buffer_read_with_doubt_kernel(tc, xb_words, xb_scales, wa, ga, offs, offs2, out):
+    nc = tc.nc
+    with ExitStack() as ctx:
+        keep = ctx.enter_context(tc.tile_pool(name="keep", bufs=1))
+        psum = ctx.enter_context(tc.psum_pool(name="psum", bufs=1))
+
+        first = keep.tile([P, T // 16], U16, name="first")
+        second = keep.tile([P, T // 16], U16, name="second")
+        x_codes = [keep.tile([P, S * PACK], U8, name=f"x_codes{g}", align_bytes=64) for g in range(PASSES)]
+        x_scales = keep.tile([P, PASSES * S], U8, name="x_scales", align_bytes=64)
+        identity = keep.tile([P, P], F32, name="identity")
+        ga_cols = keep.tile([P, PACK], F32, name="ga_cols")
+        warm = keep.tile([P, 2], F32, name="warm")
+
+        raw = {}
+
+        def load_w(g, j):
+            raw[g, j] = keep.tile([P, PACK, P], F32, name=f"raw{g}_{j}")
+            rows = wa[g * K_PASS:(g + 1) * K_PASS, j * P:(j + 1) * P]
+            nc.sync.dma_start(out=raw[g, j][:], in_=rows.rearrange("(p t) n -> p t n", t=PACK))
+
+        scale_rows = xb_scales.bitcast(I32).rearrange("g (q r) c -> r q g c", r=4)
+        planes = x_scales[:].bitcast(I32).rearrange("p (g c) -> p g c", g=PASSES)
+        for r in range(4):
+            nc.scalar.dma_start(out=planes[r:P:32], in_=scale_rows[r])
+        nc.gpsimd.memset(warm[:, 0:1], 1.0)
+        nc.scalar.activation(warm[:, 1:2], warm[:, 0:1], ACT.Abs_reciprocal_sqrt)
+
+        for g in range(PASSES):
+            load_w(g, 0)
+        for g in range(PASSES):
+            nc.sync.dma_start(
+                out=x_codes[g][:].bitcast(I32),
+                in_=xb_words[g].rearrange("p c t -> p (c t)").bitcast(I32),
+            )
+        for g in range(PASSES):
+            load_w(g, 1)
+        nc.sync.dma_start(first[:], offs)
+        nc.sync.dma_start(second[:], offs2)
+        for j in range(2, BLOCKS):
+            for g in range(PASSES):
+                load_w(g, j)
+        nc.sync.dma_start(out=ga_cols[:], in_=ga.rearrange("o (p c) -> (o p) c", c=PACK))
+        make_identity(nc, identity[:])
+
+        grouped = [keep.tile([P, PASSES * K_PASS], BF16, name=f"grouped{j}", tag=f"grouped{j}", align_bytes=64) for j in range(BLOCKS)]
+        w_codes = [keep.tile([P, PASSES * P], U32, name=f"w_codes{j}", align_bytes=64) for j in range(BLOCKS)]
+        w_scales = [keep.tile([P, PASSES * P], U8, name=f"w_scales{j}", align_bytes=64) for j in range(BLOCKS)]
+        z = [keep.tile([P, S], F32, name=f"z{j}") for j in range(BLOCKS)]
+        a = [keep.tile([P, T], F32, name=f"a{j}") for j in range(BLOCKS)]
+        ag = [keep.tile([P, T], F32, name=f"ag{j}") for j in range(BLOCKS)]
+        v = [keep.tile([P, T], F32, name=f"v{j}") for j in range(BLOCKS)]
+        d = {}
+
+        def cast(j, g, copy):
+            dst = grouped[j][:, g * K_PASS:(g + 1) * K_PASS].rearrange("p (c i t) -> p c t i", i=4, t=PACK)
+            src = raw[g, j][:].rearrange("p t (c i) -> p c t i", i=4)
+            copy(dst, src)
+
+        def quantize(j, g0, g1):
+            nc.vector.quantize_mx(
+                out=w_codes[j][:, g0 * P:g1 * P].bitcast(FP8X4),
+                scales=w_scales[j][:, g0 * P:g1 * P],
+                in_=grouped[j][:, g0 * K_PASS:g1 * K_PASS],
+            )
+
+        def one_pass(acc, j, g, lo, hi):
+            nc.tensor.matmul_mx(
+                out=acc,
+                lhsT=w_codes[j][:, g * P:(g + 1) * P].bitcast(FP8X4),
+                lhsT_scale=w_scales[j][:, g * P:(g + 1) * P],
+                rhs=x_codes[g][:, lo * PACK:hi * PACK].bitcast(FP8X4),
+                rhs_scale=x_scales[:, g * S + lo:g * S + hi],
+                start=(g == 0),
+                stop=(g == PASSES - 1),
+            )
+
+        def product(j):
+            acc = psum.tile([P, S], F32, name=f"acc{j}")
+            for g in range(PASSES):
+                one_pass(acc[:], j, g, 0, S)
+            nc.scalar.copy(z[j][:], acc[:])
+
+        def first_product():
+            width = S // 2
+            accs = [psum.tile([P, width], F32, name=f"acc0_{h}") for h in range(2)]
+            for g in range(PASSES):
+                for h in range(2):
+                    one_pass(accs[h][:], 0, g, h * width, (h + 1) * width)
+            nc.scalar.copy(z[0][:, :width], accs[0][:])
+            nc.vector.tensor_copy(z[0][:, width:], accs[1][:])
+
+        def gather_first(j):
+            for cols, entries in HALVES:
+                nc.vector.tensor_copy(a[j][:, cols], z[j][:].indirect(first[:, entries]))
+
+        def gap_tile(j):
+            tag = f"grouped{j + 2}" if j + 2 < BLOCKS else f"d{j}"
+            d[j] = keep.tile([P, T], F32, name=f"d{j}", tag=tag, align_bytes=64)
+
+        def gather_gap(j):
+            gap_tile(j)
+            for cols, entries in HALVES:
+                nc.vector.tensor_tensor(d[j][:, cols], z[j][:].indirect(second[:, entries]), a[j][:, cols], ALU.subtract)
+
+        def doubt(j):
+            u = keep.tile([P, T], F32, name=f"u{j}")
+            s = keep.tile([P, T], F32, name=f"s{j}")
+            for cols, entries in HALVES:
+                nc.scalar.activation(u[:, cols], d[j][:, cols], ACT.Abs)
+            for cols, entries in HALVES:
+                nc.scalar.activation(s[:, cols], u[:, cols], ACT.Abs_reciprocal_sqrt, bias=1.0)
+            for cols, entries in HALVES:
+                nc.scalar.activation(v[j][:, cols], s[:, cols], ACT.Square)
+
+        ga_bank = psum.tile([P, T], F32, name="ga_bank")
+
+        def spread_ga():
+            for c in range(PACK):
+                nc.tensor.transpose(ga_bank[:, c:T:PACK], ga_cols[:, c:c + 1].to_broadcast([P, P]), identity[:])
+
+        def weigh(j):
+            nc.vector.tensor_tensor(ag[j][:], a[j][:], ga_bank[:], ALU.mult)
+
+        def finish(j):
+            y = keep.tile([P, T], F32, name=f"y{j}")
+            rows = out[j * P:(j + 1) * P, :]
+            if j + 1 < BLOCKS:
+                nc.vector.tensor_tensor(y[:], ag[j][:], v[j][:], ALU.mult)
+                nc.sync.dma_start(out=rows, in_=y[:])
+            else:
+                for cols, entries in HALVES:
+                    nc.vector.tensor_tensor(y[:, cols], ag[j][:, cols], v[j][:, cols], ALU.mult)
+                    nc.sync.dma_start(out=rows[:, cols], in_=y[:, cols])
+
+        for g in range(PASSES):
+            cast(0, g, nc.vector.tensor_copy)
+        for g in range(PASSES):
+            quantize(0, g, g + 1)
+        first_product()
+        for g in range(PASSES):
+            cast(1, g, nc.vector.tensor_copy)
+        quantize(1, 0, PASSES)
+        product(1)
+        for j in range(2, BLOCKS):
+            for g in range(PASSES):
+                cast(j, g, nc.scalar.copy)
+            quantize(j, 0, PASSES)
+            product(j)
+        spread_ga()
+        for j in range(BLOCKS):
+            gather_first(j)
+            gather_gap(j)
+        for j in range(BLOCKS):
+            doubt(j)
+            weigh(j)
+            finish(j)

@@ -23,6 +23,7 @@ PASSES = K // K_PASS
 BLOCKS = N // P
 HALF = T // 2
 LIST_COLS = HALF // 16
+WINDOW = 4 * S
 HALVES = [(slice(h * HALF, (h + 1) * HALF), slice(h * LIST_COLS, (h + 1) * LIST_COLS)) for h in range(2)]
 
 
@@ -37,7 +38,7 @@ def tile_moe_buffer_read_with_doubt_kernel(tc, xb_words, xb_scales, wa, ga, offs
         x_codes = [keep.tile([P, S * PACK], U8, name=f"x_codes{g}", align_bytes=64) for g in range(PASSES)]
         x_scales = keep.tile([P, PASSES * S], U8, name="x_scales", align_bytes=64)
         identity = keep.tile([P, P], F32, name="identity")
-        ga_cols = keep.tile([P, PACK], F32, name="ga_cols")
+        ga_cols = keep.tile([P, PACK], F32, name="ga_cols", tag="ga_cols", align_bytes=64)
         warm = keep.tile([P, 2], F32, name="warm")
 
         raw = {}
@@ -49,47 +50,62 @@ def tile_moe_buffer_read_with_doubt_kernel(tc, xb_words, xb_scales, wa, ga, offs
 
         scale_rows = xb_scales.bitcast(I32).rearrange("g (q r) c -> r q g c", r=4)
         planes = x_scales[:].bitcast(I32).rearrange("p (g c) -> p g c", g=PASSES)
-        for r in range(4):
+        for r in range(2):
             nc.scalar.dma_start(out=planes[r:P:32], in_=scale_rows[r])
         nc.gpsimd.memset(warm[:, 0:1], 1.0)
         nc.scalar.activation(warm[:, 1:2], warm[:, 0:1], ACT.Abs_reciprocal_sqrt)
 
-        for g in range(PASSES):
-            load_w(g, 0)
+        load_w(0, 0)
+        for r in range(2, 4):
+            nc.sync.dma_start(out=planes[r:P:32], in_=scale_rows[r])
+        load_w(1, 0)
         for g in range(PASSES):
             nc.sync.dma_start(
                 out=x_codes[g][:].bitcast(I32),
                 in_=xb_words[g].rearrange("p c t -> p (c t)").bitcast(I32),
             )
+        nc.sync.dma_start(out=ga_cols[:], in_=ga.rearrange("o (p c) -> (o p) c", c=PACK))
+        nc.sync.dma_start(first[:], offs)
         for g in range(PASSES):
             load_w(g, 1)
-        nc.sync.dma_start(first[:], offs)
         nc.sync.dma_start(second[:], offs2)
         for j in range(2, BLOCKS):
             for g in range(PASSES):
                 load_w(g, j)
-        nc.sync.dma_start(out=ga_cols[:], in_=ga.rearrange("o (p c) -> (o p) c", c=PACK))
         make_identity(nc, identity[:])
 
-        grouped = [keep.tile([P, PASSES * K_PASS], BF16, name=f"grouped{j}", tag=f"grouped{j}", align_bytes=64) for j in range(BLOCKS)]
-        w_codes = [keep.tile([P, PASSES * P], U32, name=f"w_codes{j}", align_bytes=64) for j in range(BLOCKS)]
-        w_scales = [keep.tile([P, PASSES * P], U8, name=f"w_scales{j}", align_bytes=64) for j in range(BLOCKS)]
-        z = [keep.tile([P, S], F32, name=f"z{j}") for j in range(BLOCKS)]
-        a = [keep.tile([P, T], F32, name=f"a{j}") for j in range(BLOCKS)]
-        ag = [keep.tile([P, T], F32, name=f"ag{j}") for j in range(BLOCKS)]
-        v = [keep.tile([P, T], F32, name=f"v{j}") for j in range(BLOCKS)]
-        d = {}
+        ga_bank = psum.tile([P, T], F32, name="ga_bank")
+        grouped = {}
+        w_codes = {}
+        w_scales = {}
+        z = {}
+        ga_rows = keep.tile([P, T], F32, name="ga_rows")
+        a = {}
+        ag = {}
+        v = {}
 
-        def cast(j, g, copy):
-            dst = grouped[j][:, g * K_PASS:(g + 1) * K_PASS].rearrange("p (c i t) -> p c t i", i=4, t=PACK)
+        def wide(name, tag):
+            return keep.tile([P, T], F32, name=name, tag=tag, align_bytes=64)
+
+        def window(j, tag):
+            return keep.tile([P, WINDOW if j in (1, 2) else S], F32, name=f"z{j}", tag=tag, align_bytes=64)
+
+        def operand_tiles(j, tag, codes_tag, scales_tag):
+            if j + 1 < BLOCKS:
+                grouped[j] = keep.tile([P, PASSES * K_PASS], BF16, name=f"grouped{j}", tag=tag, align_bytes=64)
+            w_codes[j] = keep.tile([P, PASSES * P], U32, name=f"w_codes{j}", tag=codes_tag, align_bytes=64)
+            w_scales[j] = keep.tile([P, PASSES * P], U8, name=f"w_scales{j}", tag=scales_tag, align_bytes=64)
+
+        def cast(j, g, copy, into):
+            dst = into.rearrange("p (c i t) -> p c t i", i=4, t=PACK)
             src = raw[g, j][:].rearrange("p t (c i) -> p c t i", i=4)
             copy(dst, src)
 
-        def quantize(j, g0, g1):
+        def quantize(j, g0, g1, values):
             nc.vector.quantize_mx(
                 out=w_codes[j][:, g0 * P:g1 * P].bitcast(FP8X4),
                 scales=w_scales[j][:, g0 * P:g1 * P],
-                in_=grouped[j][:, g0 * K_PASS:g1 * K_PASS],
+                in_=values,
             )
 
         def one_pass(acc, j, g, lo, hi):
@@ -104,82 +120,156 @@ def tile_moe_buffer_read_with_doubt_kernel(tc, xb_words, xb_scales, wa, ga, offs
             )
 
         def product(j):
-            acc = psum.tile([P, S], F32, name=f"acc{j}")
+            acc = psum.tile([P, S], F32, name=f"acc{j}", tag=f"acc{(j + 1) % 3}")
             for g in range(PASSES):
                 one_pass(acc[:], j, g, 0, S)
-            nc.scalar.copy(z[j][:], acc[:])
+            return acc
+
+        def evacuate(j, acc, tag):
+            z[j] = window(j, tag)
+            nc.scalar.copy(z[j][:, :S], acc[:])
 
         def first_product():
             width = S // 2
-            accs = [psum.tile([P, width], F32, name=f"acc0_{h}") for h in range(2)]
+            accs = [psum.tile([P, width], F32, name=f"acc0_{h}", tag=f"acc{h}") for h in range(2)]
             for g in range(PASSES):
                 for h in range(2):
                     one_pass(accs[h][:], 0, g, h * width, (h + 1) * width)
-            nc.scalar.copy(z[0][:, :width], accs[0][:])
-            nc.vector.tensor_copy(z[0][:, width:], accs[1][:])
+            z[0] = window(0, "z0")
+            nc.vector.tensor_copy(z[0][:, :width], accs[0][:])
+            nc.vector.tensor_copy(z[0][:, width:S], accs[1][:])
 
-        def gather_first(j):
+        def gather_first(j, h, into):
+            cols, entries = HALVES[h]
+            a[j, h] = into
+            nc.vector.tensor_copy(into, z[j][:].indirect(first[:, entries]))
+
+        def gather_whole(j, tag):
+            both = wide(f"a{j}", tag)
+            for h, (cols, entries) in enumerate(HALVES):
+                gather_first(j, h, both[:, cols])
+            return both
+
+        def turned_gap(j, both, tag):
+            minus_b = wide(f"minus_b{j}", tag)
+            nc.vector.tensor_scalar(minus_b[:], z[j][:].indirect(second[:]), -1.0, 0.0, ALU.mult, ALU.add)
+            bank = psum.tile([P, T], F32, name=f"gap{j}")
+            tiles = T // P
+            for i, term in enumerate((both, minus_b)):
+                for c in range(tiles):
+                    cols = slice(c * P, (c + 1) * P)
+                    nc.tensor.matmul(bank[:, cols], term[:, cols], identity[:], start=(i == 0 and c == 0),
+                                     stop=(i == 1 and c == tiles - 1), is_transpose=True)
+            return bank
+
+        def plain_gap(j):
+            d = wide(f"d{j}", f"d{j}")
+            for h, (cols, entries) in enumerate(HALVES):
+                nc.vector.tensor_tensor(d[:, cols], z[j][:].indirect(second[:, entries]), a[j, h], ALU.subtract)
+            return d
+
+        def root(j, gap, tag):
+            u = wide(f"u{j}", tag)
+            s = wide(f"s{j}", f"s{j}")
             for cols, entries in HALVES:
-                nc.vector.tensor_copy(a[j][:, cols], z[j][:].indirect(first[:, entries]))
-
-        def gap_tile(j):
-            tag = f"grouped{j + 2}" if j + 2 < BLOCKS else f"d{j}"
-            d[j] = keep.tile([P, T], F32, name=f"d{j}", tag=tag, align_bytes=64)
-
-        def gather_gap(j):
-            gap_tile(j)
-            for cols, entries in HALVES:
-                nc.vector.tensor_tensor(d[j][:, cols], z[j][:].indirect(second[:, entries]), a[j][:, cols], ALU.subtract)
-
-        def doubt(j):
-            u = keep.tile([P, T], F32, name=f"u{j}")
-            s = keep.tile([P, T], F32, name=f"s{j}")
-            for cols, entries in HALVES:
-                nc.scalar.activation(u[:, cols], d[j][:, cols], ACT.Abs)
+                nc.scalar.activation(u[:, cols], gap[:, cols], ACT.Abs)
             for cols, entries in HALVES:
                 nc.scalar.activation(s[:, cols], u[:, cols], ACT.Abs_reciprocal_sqrt, bias=1.0)
+            return s
+
+        def square(j, s):
+            v[j] = wide(f"v{j}", f"v{j}")
             for cols, entries in HALVES:
                 nc.scalar.activation(v[j][:, cols], s[:, cols], ACT.Square)
 
-        ga_bank = psum.tile([P, T], F32, name="ga_bank")
+        def turn_back(j):
+            bank = psum.tile([P, T], F32, name=f"back{j}")
+            for c in range(T // P):
+                cols = slice(c * P, (c + 1) * P)
+                nc.tensor.transpose(bank[:, cols], v[j][:, cols], identity[:])
+            v[j] = bank
 
         def spread_ga():
             for c in range(PACK):
                 nc.tensor.transpose(ga_bank[:, c:T:PACK], ga_cols[:, c:c + 1].to_broadcast([P, P]), identity[:])
+            nc.scalar.copy(ga_rows[:], ga_bank[:])
 
-        def weigh(j):
-            nc.vector.tensor_tensor(ag[j][:], a[j][:], ga_bank[:], ALU.mult)
-
-        def finish(j):
-            y = keep.tile([P, T], F32, name=f"y{j}")
+        def finish(j, tag):
+            y = wide(f"y{j}", tag)
             rows = out[j * P:(j + 1) * P, :]
-            if j + 1 < BLOCKS:
-                nc.vector.tensor_tensor(y[:], ag[j][:], v[j][:], ALU.mult)
-                nc.sync.dma_start(out=rows, in_=y[:])
-            else:
-                for cols, entries in HALVES:
-                    nc.vector.tensor_tensor(y[:, cols], ag[j][:, cols], v[j][:, cols], ALU.mult)
-                    nc.sync.dma_start(out=rows[:, cols], in_=y[:, cols])
+            nc.vector.tensor_tensor(y[:], ag[j][:], v[j][:], ALU.mult)
+            nc.sync.dma_start(out=rows, in_=y[:])
 
+        def finish_halves(j, tag, weighed):
+            y = wide(f"y{j}", tag)
+            rows = out[j * P:(j + 1) * P, :]
+            for h, (cols, entries) in enumerate(HALVES):
+                nc.vector.tensor_tensor(y[:, cols], weighed[h], v[j][:, cols], ALU.mult)
+                nc.sync.dma_start(out=rows[:, cols], in_=y[:, cols])
+
+        def half_tile(name, tag):
+            return keep.tile([P, HALF], F32, name=name, tag=tag, align_bytes=64)
+
+        def pass_cols(g):
+            return slice(g * K_PASS, (g + 1) * K_PASS)
+
+        operand_tiles(0, "grouped0", "w_codes0", "w_scales0")
         for g in range(PASSES):
-            cast(0, g, nc.vector.tensor_copy)
+            cast(0, g, nc.vector.tensor_copy, grouped[0][:, pass_cols(g)])
         for g in range(PASSES):
-            quantize(0, g, g + 1)
+            quantize(0, g, g + 1, grouped[0][:, pass_cols(g)])
         first_product()
-        for g in range(PASSES):
-            cast(1, g, nc.vector.tensor_copy)
-        quantize(1, 0, PASSES)
-        product(1)
-        for j in range(2, BLOCKS):
-            for g in range(PASSES):
-                cast(j, g, nc.scalar.copy)
-            quantize(j, 0, PASSES)
-            product(j)
         spread_ga()
-        for j in range(BLOCKS):
-            gather_first(j)
-            gather_gap(j)
-        for j in range(BLOCKS):
-            doubt(j)
-            weigh(j)
-            finish(j)
+        operand_tiles(1, "grouped1", "w_codes1", "ga_cols")
+        for g in range(PASSES):
+            cast(1, g, nc.scalar.copy, grouped[1][:, pass_cols(g)])
+        gather_first(0, 0, half_tile("a0_0", "a0_0")[:])
+        quantize(1, 0, PASSES, grouped[1][:])
+        evacuate(1, product(1), "z1")
+        operand_tiles(2, "grouped2", "z0", "w_scales2")
+        for g in range(PASSES):
+            cast(2, g, nc.scalar.copy, grouped[2][:, pass_cols(g)])
+        early = keep.tile([P, K_PASS], BF16, name="early", tag="early", align_bytes=64)
+        cast(3, 0, nc.scalar.copy, early[:])
+        late = keep.tile([P, K_PASS], BF16, name="late", tag="w_codes1", align_bytes=64)
+        cast(3, 1, nc.scalar.copy, late[:])
+        gather_first(0, 1, half_tile("a0_1", "grouped1")[:])
+        gap0 = plain_gap(0)
+        quantize(2, 0, PASSES, grouped[2][:])
+        acc2 = product(2)
+        a1 = gather_whole(1, "a1")
+        ag0 = [half_tile("ag0_0", "grouped2"), half_tile("ag0_1", "ag0_1")]
+        for h, (cols, entries) in enumerate(HALVES):
+            nc.gpsimd.tensor_tensor(ag0[h][:], a[0, h], ga_rows[:, cols], ALU.mult)
+        gap1 = turned_gap(1, a1, "minus_b1")
+        operand_tiles(3, "", "z1", "w_scales3")
+        quantize(3, 0, 1, early[:])
+        quantize(3, 1, 2, late[:])
+        acc3 = product(3)
+        ag[1] = wide("ag1", "w_codes1")
+        nc.gpsimd.tensor_tensor(ag[1][:], a1[:], ga_rows[:], ALU.mult)
+        s0 = root(0, gap0, "ga_cols")
+        evacuate(2, acc2, "ga_cols")
+        square(0, s0)
+        a2 = gather_whole(2, "a2")
+        gap2 = turned_gap(2, a2, "minus_b2")
+        ag[2] = wide("ag2", "ag2")
+        nc.gpsimd.tensor_tensor(ag[2][:], a2[:], ga_rows[:], ALU.mult)
+        s1 = root(1, gap1, "u1")
+        evacuate(3, acc3, "u1")
+        square(1, s1)
+        turn_back(1)
+        a3 = gather_whole(3, "a3")
+        gap3 = plain_gap(3)
+        square(2, root(2, gap2, "u2"))
+        turn_back(2)
+        square(3, root(3, gap3, "u3"))
+        y0 = wide("y0", "u1")
+        for h, (cols, entries) in enumerate(HALVES):
+            nc.vector.tensor_tensor(y0[:, cols], ag0[h][:], v[0][:, cols], ALU.mult)
+        nc.sync.dma_start(out=out[0:P, :], in_=y0[:])
+        finish(1, "y1")
+        ag[3] = wide("ag3", "ag3")
+        nc.vector.tensor_tensor(ag[3][:], a3[:], ga_bank[:], ALU.mult)
+        finish(2, "y2")
+        finish_halves(3, "y3", [ag[3][:, cols] for cols, entries in HALVES])

@@ -44,7 +44,7 @@ def tile_moe_buffer_read_with_doubt_kernel(tc, xb_words, xb_scales, wa, ga, offs
         raw = {}
 
         def load_w(g, j):
-            raw[g, j] = keep.tile([P, PACK, P], F32, name=f"raw{g}_{j}")
+            raw[g, j] = keep.tile([P, PACK, P], F32, name=f"raw{g}_{j}", tag=f"raw{g}_{j}", align_bytes=64)
             rows = wa[g * K_PASS:(g + 1) * K_PASS, j * P:(j + 1) * P]
             nc.sync.dma_start(out=raw[g, j][:], in_=rows.rearrange("(p t) n -> p t n", t=PACK))
 
@@ -59,15 +59,15 @@ def tile_moe_buffer_read_with_doubt_kernel(tc, xb_words, xb_scales, wa, ga, offs
         for r in range(2, 4):
             nc.sync.dma_start(out=planes[r:P:32], in_=scale_rows[r])
         load_w(1, 0)
-        for g in range(PASSES):
+        for g, lo, hi in ((0, 0, S), (1, 0, S)):
             nc.sync.dma_start(
-                out=x_codes[g][:].bitcast(I32),
-                in_=xb_words[g].rearrange("p c t -> p (c t)").bitcast(I32),
+                out=x_codes[g][:, lo * PACK:hi * PACK].bitcast(I32),
+                in_=xb_words[g].rearrange("p c t -> p (c t)")[:, lo * PACK:hi * PACK].bitcast(I32),
             )
-        nc.sync.dma_start(out=ga_cols[:], in_=ga.rearrange("o (p c) -> (o p) c", c=PACK))
-        nc.sync.dma_start(first[:], offs)
         for g in range(PASSES):
             load_w(g, 1)
+        nc.sync.dma_start(first[:], offs)
+        nc.sync.dma_start(out=ga_cols[:], in_=ga.rearrange("o (p c) -> (o p) c", c=PACK))
         nc.sync.dma_start(second[:], offs2)
         for j in range(2, BLOCKS):
             for g in range(PASSES):
@@ -88,7 +88,7 @@ def tile_moe_buffer_read_with_doubt_kernel(tc, xb_words, xb_scales, wa, ga, offs
             return keep.tile([P, T], F32, name=name, tag=tag, align_bytes=64)
 
         def window(j, tag):
-            return keep.tile([P, WINDOW if j in (1, 2) else S], F32, name=f"z{j}", tag=tag, align_bytes=64)
+            return keep.tile([P, WINDOW if j + 1 < BLOCKS else S], F32, name=f"z{j}", tag=tag, align_bytes=64)
 
         def operand_tiles(j, tag, codes_tag, scales_tag):
             if j + 1 < BLOCKS:
@@ -144,10 +144,15 @@ def tile_moe_buffer_read_with_doubt_kernel(tc, xb_words, xb_scales, wa, ga, offs
             a[j, h] = into
             nc.vector.tensor_copy(into, z[j][:].indirect(first[:, entries]))
 
-        def gather_whole(j, tag):
+        def gather_halves(j, tag):
             both = wide(f"a{j}", tag)
             for h, (cols, entries) in enumerate(HALVES):
                 gather_first(j, h, both[:, cols])
+            return both
+
+        def gather_whole(j, tag):
+            both = wide(f"a{j}", tag)
+            nc.vector.tensor_copy(both[:], z[j][:].indirect(first[:]))
             return both
 
         def turned_gap(j, both, tag):
@@ -162,8 +167,8 @@ def tile_moe_buffer_read_with_doubt_kernel(tc, xb_words, xb_scales, wa, ga, offs
                                      stop=(i == 1 and c == tiles - 1), is_transpose=True)
             return bank
 
-        def plain_gap(j):
-            d = wide(f"d{j}", f"d{j}")
+        def plain_gap(j, tag):
+            d = wide(f"d{j}", tag)
             for h, (cols, entries) in enumerate(HALVES):
                 nc.vector.tensor_tensor(d[:, cols], z[j][:].indirect(second[:, entries]), a[j, h], ALU.subtract)
             return d
@@ -205,7 +210,7 @@ def tile_moe_buffer_read_with_doubt_kernel(tc, xb_words, xb_scales, wa, ga, offs
             rows = out[j * P:(j + 1) * P, :]
             for h, (cols, entries) in enumerate(HALVES):
                 nc.vector.tensor_tensor(y[:, cols], weighed[h], v[j][:, cols], ALU.mult)
-                nc.sync.dma_start(out=rows[:, cols], in_=y[:, cols])
+                (nc.sync, nc.scalar)[h].dma_start(out=rows[:, cols], in_=y[:, cols])
 
         def half_tile(name, tag):
             return keep.tile([P, HALF], F32, name=name, tag=tag, align_bytes=64)
@@ -223,52 +228,53 @@ def tile_moe_buffer_read_with_doubt_kernel(tc, xb_words, xb_scales, wa, ga, offs
         operand_tiles(1, "grouped1", "w_codes1", "ga_cols")
         for g in range(PASSES):
             cast(1, g, nc.scalar.copy, grouped[1][:, pass_cols(g)])
-        gather_first(0, 0, half_tile("a0_0", "a0_0")[:])
+        a0 = gather_whole(0, "a0")
         quantize(1, 0, PASSES, grouped[1][:])
-        evacuate(1, product(1), "z1")
-        operand_tiles(2, "grouped2", "z0", "w_scales2")
-        for g in range(PASSES):
-            cast(2, g, nc.scalar.copy, grouped[2][:, pass_cols(g)])
-        early = keep.tile([P, K_PASS], BF16, name="early", tag="early", align_bytes=64)
-        cast(3, 0, nc.scalar.copy, early[:])
-        late = keep.tile([P, K_PASS], BF16, name="late", tag="w_codes1", align_bytes=64)
-        cast(3, 1, nc.scalar.copy, late[:])
-        gather_first(0, 1, half_tile("a0_1", "grouped1")[:])
-        gap0 = plain_gap(0)
-        quantize(2, 0, PASSES, grouped[2][:])
+        acc1 = product(1)
+        pair = keep.tile([P, 2, PASSES * K_PASS], BF16, name="pair", tag="pair", align_bytes=64)
+        for j in (2, 3):
+            for g in range(PASSES):
+                cast(j, g, nc.scalar.copy, pair[:, j - 2, pass_cols(g)])
+        evacuate(1, acc1, "raw1_3")
+        gap0 = wide("d0", "grouped1")
+        nc.vector.tensor_tensor(gap0[:], z[0][:].indirect(second[:]), a0[:], ALU.subtract)
+        pair_codes = keep.tile([P, 2, PASSES * P], U32, name="pair_codes", tag="z0", align_bytes=64)
+        pair_scales = keep.tile([P, 2, PASSES * P], U8, name="pair_scales", align_bytes=64)
+        nc.vector.quantize_mx(
+            out=pair_codes[:].rearrange("p j c -> p (j c)").bitcast(FP8X4),
+            scales=pair_scales[:].rearrange("p j c -> p (j c)"),
+            in_=pair[:].rearrange("p j c -> p (j c)"),
+        )
+        for j in (2, 3):
+            w_codes[j] = pair_codes[:, j - 2, :]
+            w_scales[j] = pair_scales[:, j - 2, :]
         acc2 = product(2)
         a1 = gather_whole(1, "a1")
-        ag0 = [half_tile("ag0_0", "grouped2"), half_tile("ag0_1", "ag0_1")]
-        for h, (cols, entries) in enumerate(HALVES):
-            nc.gpsimd.tensor_tensor(ag0[h][:], a[0, h], ga_rows[:, cols], ALU.mult)
-        gap1 = turned_gap(1, a1, "minus_b1")
-        operand_tiles(3, "", "z1", "w_scales3")
-        quantize(3, 0, 1, early[:])
-        quantize(3, 1, 2, late[:])
+        ag[0] = wide("ag0", "pair")
+        nc.gpsimd.tensor_tensor(ag[0][:], a0[:], ga_rows[:], ALU.mult)
         acc3 = product(3)
-        ag[1] = wide("ag1", "w_codes1")
+        gap1 = turned_gap(1, a1, "minus_b1")
+        ag[1] = wide("ag1", "ag1")
         nc.gpsimd.tensor_tensor(ag[1][:], a1[:], ga_rows[:], ALU.mult)
         s0 = root(0, gap0, "ga_cols")
         evacuate(2, acc2, "ga_cols")
         square(0, s0)
+        evacuate(3, acc3, "s0")
+        y0 = wide("y0", "y0")
+        nc.gpsimd.tensor_tensor(y0[:], ag[0][:], v[0][:], ALU.mult)
+        nc.sync.dma_start(out=out[0:P, :], in_=y0[:])
         a2 = gather_whole(2, "a2")
         gap2 = turned_gap(2, a2, "minus_b2")
-        ag[2] = wide("ag2", "ag2")
+        ag[2] = wide("ag2", "v0")
         nc.gpsimd.tensor_tensor(ag[2][:], a2[:], ga_rows[:], ALU.mult)
-        s1 = root(1, gap1, "u1")
-        evacuate(3, acc3, "u1")
-        square(1, s1)
+        square(1, root(1, gap1, "u1"))
         turn_back(1)
-        a3 = gather_whole(3, "a3")
-        gap3 = plain_gap(3)
+        a3 = gather_halves(3, "a3")
+        gap3 = plain_gap(3, "d3")
         square(2, root(2, gap2, "u2"))
         turn_back(2)
         square(3, root(3, gap3, "u3"))
-        y0 = wide("y0", "u1")
-        for h, (cols, entries) in enumerate(HALVES):
-            nc.vector.tensor_tensor(y0[:, cols], ag0[h][:], v[0][:, cols], ALU.mult)
-        nc.sync.dma_start(out=out[0:P, :], in_=y0[:])
-        finish(1, "y1")
+        finish(1, "s0")
         ag[3] = wide("ag3", "ag3")
         nc.vector.tensor_tensor(ag[3][:], a3[:], ga_bank[:], ALU.mult)
         finish(2, "y2")

@@ -91,8 +91,7 @@ def tile_moe_buffer_read_with_doubt_kernel(tc, xb_words, xb_scales, wa, ga, offs
             return keep.tile([P, WINDOW if j + 1 < BLOCKS else S], F32, name=f"z{j}", tag=tag, align_bytes=64)
 
         def operand_tiles(j, tag, codes_tag, scales_tag):
-            if j + 1 < BLOCKS:
-                grouped[j] = keep.tile([P, PASSES * K_PASS], BF16, name=f"grouped{j}", tag=tag, align_bytes=64)
+            grouped[j] = keep.tile([P, PASSES * K_PASS], BF16, name=f"grouped{j}", tag=tag, align_bytes=64)
             w_codes[j] = keep.tile([P, PASSES * P], U32, name=f"w_codes{j}", tag=codes_tag, align_bytes=64)
             w_scales[j] = keep.tile([P, PASSES * P], U8, name=f"w_scales{j}", tag=scales_tag, align_bytes=64)
 
@@ -173,13 +172,13 @@ def tile_moe_buffer_read_with_doubt_kernel(tc, xb_words, xb_scales, wa, ga, offs
                 nc.vector.tensor_tensor(d[:, cols], z[j][:].indirect(second[:, entries]), a[j, h], ALU.subtract)
             return d
 
-        def root(j, gap, tag):
-            u = wide(f"u{j}", tag)
+        def root(j, gap, tags):
+            u = [half_tile(f"u{j}_{h}", tags[h]) for h in range(2)]
             s = wide(f"s{j}", f"s{j}")
-            for cols, entries in HALVES:
-                nc.scalar.activation(u[:, cols], gap[:, cols], ACT.Abs)
-            for cols, entries in HALVES:
-                nc.scalar.activation(s[:, cols], u[:, cols], ACT.Abs_reciprocal_sqrt, bias=1.0)
+            for h, (cols, entries) in enumerate(HALVES):
+                nc.scalar.activation(u[h][:], gap[:, cols], ACT.Abs)
+            for h, (cols, entries) in enumerate(HALVES):
+                nc.scalar.activation(s[:, cols], u[h][:], ACT.Abs_reciprocal_sqrt, bias=1.0)
             return s
 
         def square(j, s):
@@ -230,34 +229,27 @@ def tile_moe_buffer_read_with_doubt_kernel(tc, xb_words, xb_scales, wa, ga, offs
             cast(1, g, nc.scalar.copy, grouped[1][:, pass_cols(g)])
         a0 = gather_whole(0, "a0")
         quantize(1, 0, PASSES, grouped[1][:])
-        acc1 = product(1)
-        pair = keep.tile([P, 2, PASSES * K_PASS], BF16, name="pair", tag="pair", align_bytes=64)
-        for j in (2, 3):
-            for g in range(PASSES):
-                cast(j, g, nc.scalar.copy, pair[:, j - 2, pass_cols(g)])
-        evacuate(1, acc1, "raw1_3")
+        operand_tiles(2, "grouped2", "z0", "w_scales2")
+        for g in range(PASSES):
+            cast(2, g, nc.scalar.copy, grouped[2][:, pass_cols(g)])
+        evacuate(1, product(1), "z1")
+        operand_tiles(3, "w_codes1", "w_codes3", "w_scales3")
+        for g in range(PASSES):
+            cast(3, g, nc.scalar.copy, grouped[3][:, pass_cols(g)])
         gap0 = wide("d0", "grouped1")
         nc.vector.tensor_tensor(gap0[:], z[0][:].indirect(second[:]), a0[:], ALU.subtract)
-        pair_codes = keep.tile([P, 2, PASSES * P], U32, name="pair_codes", tag="z0", align_bytes=64)
-        pair_scales = keep.tile([P, 2, PASSES * P], U8, name="pair_scales", align_bytes=64)
-        nc.vector.quantize_mx(
-            out=pair_codes[:].rearrange("p j c -> p (j c)").bitcast(FP8X4),
-            scales=pair_scales[:].rearrange("p j c -> p (j c)"),
-            in_=pair[:].rearrange("p j c -> p (j c)"),
-        )
-        for j in (2, 3):
-            w_codes[j] = pair_codes[:, j - 2, :]
-            w_scales[j] = pair_scales[:, j - 2, :]
+        quantize(2, 0, PASSES, grouped[2][:])
         acc2 = product(2)
-        a1 = gather_whole(1, "a1")
-        ag[0] = wide("ag0", "pair")
+        ag[0] = wide("ag0", "grouped2")
         nc.gpsimd.tensor_tensor(ag[0][:], a0[:], ga_rows[:], ALU.mult)
+        a1 = gather_whole(1, "a1")
+        quantize(3, 0, PASSES, grouped[3][:])
+        gap1 = turned_gap(1, a1, "w_codes1")
         acc3 = product(3)
-        gap1 = turned_gap(1, a1, "minus_b1")
-        ag[1] = wide("ag1", "ag1")
-        nc.gpsimd.tensor_tensor(ag[1][:], a1[:], ga_rows[:], ALU.mult)
-        s0 = root(0, gap0, "ga_cols")
-        evacuate(2, acc2, "ga_cols")
+        ag[1] = a1
+        nc.gpsimd.tensor_tensor(a1[:], a1[:], ga_rows[:], ALU.mult)
+        s0 = root(0, gap0, ("raw1_3", "ga_cols"))
+        evacuate(2, acc2, "raw1_3")
         square(0, s0)
         evacuate(3, acc3, "s0")
         y0 = wide("y0", "y0")
@@ -267,13 +259,13 @@ def tile_moe_buffer_read_with_doubt_kernel(tc, xb_words, xb_scales, wa, ga, offs
         gap2 = turned_gap(2, a2, "minus_b2")
         ag[2] = wide("ag2", "v0")
         nc.gpsimd.tensor_tensor(ag[2][:], a2[:], ga_rows[:], ALU.mult)
-        square(1, root(1, gap1, "u1"))
+        square(1, root(1, gap1, ("u1_0", "u1_1")))
         turn_back(1)
         a3 = gather_halves(3, "a3")
         gap3 = plain_gap(3, "d3")
-        square(2, root(2, gap2, "u2"))
+        square(2, root(2, gap2, ("u2_0", "u2_1")))
         turn_back(2)
-        square(3, root(3, gap3, "u3"))
+        square(3, root(3, gap3, ("u3_0", "u3_1")))
         finish(1, "s0")
         ag[3] = wide("ag3", "ag3")
         nc.vector.tensor_tensor(ag[3][:], a3[:], ga_bank[:], ALU.mult)

from contextlib import ExitStack

import concourse.mybir as mybir
from concourse.masks import make_identity

K, S, T, N = 1024, 512, 512, 512
FLOPS = 2 * K * S * N

F32 = mybir.dt.float32
BF16 = mybir.dt.bfloat16
I32 = mybir.dt.int32
U32 = mybir.dt.uint32
U16 = mybir.dt.uint16
U8 = mybir.dt.uint8
FP8X4 = mybir.dt.float8_e4m3fn_x4
ACT = mybir.ActivationFunctionType
ALU = mybir.AluOpType

P = 128
PACK = 4
K_PASS = P * PACK
PASSES = K // K_PASS
BLOCKS = N // P
HALF = T // 2
LIST_COLS = HALF // 16
WINDOW = 4 * S
HALVES = [(slice(h * HALF, (h + 1) * HALF), slice(h * LIST_COLS, (h + 1) * LIST_COLS)) for h in range(2)]


def tile_moe_buffer_read_with_doubt_kernel(tc, xb_words, xb_scales, wa, ga, offs, offs2, out):
    nc = tc.nc
    with ExitStack() as ctx:
        keep = ctx.enter_context(tc.tile_pool(name="keep", bufs=1))
        psum = ctx.enter_context(tc.psum_pool(name="psum", bufs=1))

        first = keep.tile([P, T // 16], U16, name="first")
        second = keep.tile([P, T // 16], U16, name="second")
        x_codes = [keep.tile([P, S * PACK], U8, name=f"x_codes{g}", align_bytes=64) for g in range(PASSES)]
        x_scales = keep.tile([P, PASSES * S], U8, name="x_scales", align_bytes=64)
        identity = keep.tile([P, P], F32, name="identity")
        ga_cols = keep.tile([P, PACK], F32, name="ga_cols", tag="ga_cols", align_bytes=64)
        warm = keep.tile([P, 2], F32, name="warm")

        raw = {}

        def load_w(g, j):
            raw[g, j] = keep.tile([P, PACK, P], F32, name=f"raw{g}_{j}", tag=f"raw{g}_{j}", align_bytes=64)
            rows = wa[g * K_PASS:(g + 1) * K_PASS, j * P:(j + 1) * P]
            nc.sync.dma_start(out=raw[g, j][:], in_=rows.rearrange("(p t) n -> p t n", t=PACK))

        scale_rows = xb_scales.bitcast(I32).rearrange("g (q r) c -> r q g c", r=4)
        planes = x_scales[:].bitcast(I32).rearrange("p (g c) -> p g c", g=PASSES)
        for r in range(2):
            nc.scalar.dma_start(out=planes[r:P:32], in_=scale_rows[r])
        nc.gpsimd.memset(warm[:, 0:1], 1.0)
        nc.scalar.activation(warm[:, 1:2], warm[:, 0:1], ACT.Abs_reciprocal_sqrt)

        load_w(0, 0)
        for r in range(2, 4):
            nc.sync.dma_start(out=planes[r:P:32], in_=scale_rows[r])
        load_w(1, 0)
        for g, lo, hi in ((0, 0, S), (1, 0, S)):
            nc.sync.dma_start(
                out=x_codes[g][:, lo * PACK:hi * PACK].bitcast(I32),
                in_=xb_words[g].rearrange("p c t -> p (c t)")[:, lo * PACK:hi * PACK].bitcast(I32),
            )
        for g in range(PASSES):
            load_w(g, 1)
        nc.sync.dma_start(first[:], offs)
        nc.sync.dma_start(out=ga_cols[:], in_=ga.rearrange("o (p c) -> (o p) c", c=PACK))
        nc.sync.dma_start(second[:], offs2)
        for j in range(2, BLOCKS):
            for g in range(PASSES):
                load_w(g, j)
        make_identity(nc, identity[:])

        ga_bank = psum.tile([P, T], F32, name="ga_bank")
        grouped = {}
        w_codes = {}
        w_scales = {}
        z = {}
        ga_rows = keep.tile([P, T], F32, name="ga_rows")
        a = {}
        ag = {}
        v = {}

        def wide(name, tag):
            return keep.tile([P, T], F32, name=name, tag=tag, align_bytes=64)

        def window(j, tag):
            return keep.tile([P, WINDOW if j + 1 < BLOCKS else S], F32, name=f"z{j}", tag=tag, align_bytes=64)

        def operand_tiles(j, tag, codes_tag, scales_tag):
            grouped[j] = keep.tile([P, PASSES * K_PASS], BF16, name=f"grouped{j}", tag=tag, align_bytes=64)
            w_codes[j] = keep.tile([P, PASSES * P], U32, name=f"w_codes{j}", tag=codes_tag, align_bytes=64)
            w_scales[j] = keep.tile([P, PASSES * P], U8, name=f"w_scales{j}", tag=scales_tag, align_bytes=64)

        def cast(j, g, copy, into):
            dst = into.rearrange("p (c i t) -> p c t i", i=4, t=PACK)
            src = raw[g, j][:].rearrange("p t (c i) -> p c t i", i=4)
            copy(dst, src)

        def quantize(j, g0, g1, values):
            nc.vector.quantize_mx(
                out=w_codes[j][:, g0 * P:g1 * P].bitcast(FP8X4),
                scales=w_scales[j][:, g0 * P:g1 * P],
                in_=values,
            )

        def one_pass(acc, j, g, lo, hi):
            nc.tensor.matmul_mx(
                out=acc,
                lhsT=w_codes[j][:, g * P:(g + 1) * P].bitcast(FP8X4),
                lhsT_scale=w_scales[j][:, g * P:(g + 1) * P],
                rhs=x_codes[g][:, lo * PACK:hi * PACK].bitcast(FP8X4),
                rhs_scale=x_scales[:, g * S + lo:g * S + hi],
                start=(g == 0),
                stop=(g == PASSES - 1),
            )

        def product(j):
            acc = psum.tile([P, S], F32, name=f"acc{j}", tag=f"acc{(j + 1) % 3}")
            for g in range(PASSES):
                one_pass(acc[:], j, g, 0, S)
            return acc

        def evacuate(j, acc, tag):
            z[j] = window(j, tag)
            nc.scalar.copy(z[j][:, :S], acc[:])

        def first_product():
            width = S // 2
            accs = [psum.tile([P, width], F32, name=f"acc0_{h}", tag=f"acc{h}") for h in range(2)]
            for g in range(PASSES):
                for h in range(2):
                    one_pass(accs[h][:], 0, g, h * width, (h + 1) * width)
            z[0] = window(0, "z0")
            nc.vector.tensor_copy(z[0][:, :width], accs[0][:])
            nc.vector.tensor_copy(z[0][:, width:S], accs[1][:])

        def gather_first(j, h, into):
            cols, entries = HALVES[h]
            a[j, h] = into
            nc.vector.tensor_copy(into, z[j][:].indirect(first[:, entries]))

        def gather_halves(j, tag):
            both = wide(f"a{j}", tag)
            for h, (cols, entries) in enumerate(HALVES):
                gather_first(j, h, both[:, cols])
            return both

        def gather_whole(j, tag):
            both = wide(f"a{j}", tag)
            nc.vector.tensor_copy(both[:], z[j][:].indirect(first[:]))
            return both

        def turned_gap(j, both, tag):
            minus_b = wide(f"minus_b{j}", tag)
            nc.vector.tensor_scalar(minus_b[:], z[j][:].indirect(second[:]), -1.0, 0.0, ALU.mult, ALU.add)
            bank = psum.tile([P, T], F32, name=f"gap{j}")
            tiles = T // P
            for i, term in enumerate((both, minus_b)):
                for c in range(tiles):
                    cols = slice(c * P, (c + 1) * P)
                    nc.tensor.matmul(bank[:, cols], term[:, cols], identity[:], start=(i == 0 and c == 0),
                                     stop=(i == 1 and c == tiles - 1), is_transpose=True)
            return bank

        def plain_gap(j, tag):
            d = wide(f"d{j}", tag)
            for h, (cols, entries) in enumerate(HALVES):
                nc.vector.tensor_tensor(d[:, cols], z[j][:].indirect(second[:, entries]), a[j, h], ALU.subtract)
            return d

        def root(j, gap, tags):
            u = [half_tile(f"u{j}_{h}", tags[h]) for h in range(2)]
            s = wide(f"s{j}", f"s{j}")
            for h, (cols, entries) in enumerate(HALVES):
                nc.scalar.activation(u[h][:], gap[:, cols], ACT.Abs)
            for h, (cols, entries) in enumerate(HALVES):
                nc.scalar.activation(s[:, cols], u[h][:], ACT.Abs_reciprocal_sqrt, bias=1.0)
            return s

        def square(j, s):
            v[j] = wide(f"v{j}", f"v{j}")
            for cols, entries in HALVES:
                nc.scalar.activation(v[j][:, cols], s[:, cols], ACT.Square)

        def turn_back(j):
            bank = psum.tile([P, T], F32, name=f"back{j}")
            for c in range(T // P):
                cols = slice(c * P, (c + 1) * P)
                nc.tensor.transpose(bank[:, cols], v[j][:, cols], identity[:])
            v[j] = bank

        def spread_ga():
            for c in range(PACK):
                nc.tensor.transpose(ga_bank[:, c:T:PACK], ga_cols[:, c:c + 1].to_broadcast([P, P]), identity[:])
            nc.scalar.copy(ga_rows[:], ga_bank[:])

        def finish(j, tag):
            y = wide(f"y{j}", tag)
            rows = out[j * P:(j + 1) * P, :]
            nc.vector.tensor_tensor(y[:], ag[j][:], v[j][:], ALU.mult)
            nc.sync.dma_start(out=rows, in_=y[:])

        def finish_halves(j, tag, weighed):
            y = wide(f"y{j}", tag)
            rows = out[j * P:(j + 1) * P, :]
            for h, (cols, entries) in enumerate(HALVES):
                nc.vector.tensor_tensor(y[:, cols], weighed[h], v[j][:, cols], ALU.mult)
                (nc.sync, nc.scalar)[h].dma_start(out=rows[:, cols], in_=y[:, cols])

        def half_tile(name, tag):
            return keep.tile([P, HALF], F32, name=name, tag=tag, align_bytes=64)

        def pass_cols(g):
            return slice(g * K_PASS, (g + 1) * K_PASS)

        operand_tiles(0, "grouped0", "w_codes0", "w_scales0")
        for g in range(PASSES):
            cast(0, g, nc.vector.tensor_copy, grouped[0][:, pass_cols(g)])
        for g in range(PASSES):
            quantize(0, g, g + 1, grouped[0][:, pass_cols(g)])
        first_product()
        spread_ga()
        operand_tiles(1, "grouped1", "w_codes1", "ga_cols")
        for g in range(PASSES):
            cast(1, g, nc.scalar.copy, grouped[1][:, pass_cols(g)])
        a0 = gather_whole(0, "a0")
        quantize(1, 0, PASSES, grouped[1][:])
        operand_tiles(2, "grouped2", "z0", "w_scales2")
        for g in range(PASSES):
            cast(2, g, nc.scalar.copy, grouped[2][:, pass_cols(g)])
        evacuate(1, product(1), "z1")
        operand_tiles(3, "w_codes1", "w_codes3", "w_scales3")
        for g in range(PASSES):
            cast(3, g, nc.scalar.copy, grouped[3][:, pass_cols(g)])
        gap0 = wide("d0", "grouped1")
        nc.vector.tensor_tensor(gap0[:], z[0][:].indirect(second[:]), a0[:], ALU.subtract)
        quantize(2, 0, PASSES, grouped[2][:])
        acc2 = product(2)
        ag[0] = wide("ag0", "grouped2")
        nc.gpsimd.tensor_tensor(ag[0][:], a0[:], ga_rows[:], ALU.mult)
        a1 = gather_whole(1, "a1")
        quantize(3, 0, PASSES, grouped[3][:])
        gap1 = turned_gap(1, a1, "w_codes1")
        acc3 = product(3)
        ag[1] = a1
        nc.gpsimd.tensor_tensor(a1[:], a1[:], ga_rows[:], ALU.mult)
        s0 = root(0, gap0, ("raw1_3", "ga_cols"))
        evacuate(2, acc2, "raw1_3")
        square(0, s0)
        evacuate(3, acc3, "s0")
        y0 = wide("y0", "y0")
        nc.gpsimd.tensor_tensor(y0[:], ag[0][:], v[0][:], ALU.mult)
        nc.sync.dma_start(out=out[0:P, :], in_=y0[:])
        a2 = gather_whole(2, "a2")
        gap2 = turned_gap(2, a2, "minus_b2")
        ag[2] = wide("ag2", "v0")
        nc.gpsimd.tensor_tensor(ag[2][:], a2[:], ga_rows[:], ALU.mult)
        square(1, root(1, gap1, ("u1_0", "u1_1")))
        turn_back(1)
        a3 = gather_halves(3, "a3")
        gap3 = plain_gap(3, "d3")
        square(2, root(2, gap2, ("u2_0", "u2_1")))
        turn_back(2)
        square(3, root(3, gap3, ("u3_0", "u3_1")))
        finish(1, "s0")
        ag[3] = wide("ag3", "ag3")
        nc.vector.tensor_tensor(ag[3][:], a3[:], ga_bank[:], ALU.mult)
        finish(2, "y2")
        finish_halves(3, "y3", [ag[3][:, cols] for cols, entries in HALVES])
